import numpy as np
import ml_dtypes


def mxq(x, axis, fmt="e4m3"):
    dtype, down = {"e4m3": (ml_dtypes.float8_e4m3fn, 7), "e5m2": (ml_dtypes.float8_e5m2, 14)}[fmt]
    v = np.moveaxis(np.asarray(x, np.float32).astype(ml_dtypes.bfloat16).astype(np.float64), axis, -1)
    blocks = v.reshape(v.shape[:-1] + (-1, 32))
    amax = np.abs(blocks).max(-1, keepdims=True)
    byte = np.maximum(np.where(amax > 0, np.frexp(amax)[1] - 1 + 127, 0) - down, 1)
    scale = np.exp2(byte - 127.0)
    codes = (blocks / scale).astype(np.float32).astype(dtype).astype(np.float64)
    return np.moveaxis((codes * scale).reshape(v.shape), -1, axis)


WIDE = False


def mx_kscale(k):
    if not WIDE:
        return np.ones(k)
    levels = np.array([10, -10, 5, -5, 0])
    if k % 512:
        return np.exp2(np.random.permutation(np.resize(levels, k // 32))).repeat(32)
    a = np.empty((k // 512, 16))
    for p in range(k // 512):
        a[p, :8] = np.random.permutation(np.resize(levels, 8))
        for g in range(8):
            far = levels[np.abs(levels - a[p, g]) >= 10]
            a[p, g + 8] = far[np.random.randint(len(far))]
    return np.exp2(a.ravel()).repeat(32)


def f64(x):
    return np.asarray(x).astype(np.float64)


def striped(idx):
    return np.tile(idx.reshape(-1, 16).T, (8, 1)).astype(np.uint16)


def unstriped(offs):
    return offs[:16].T.reshape(-1).astype(np.int64)


def striped8(idx):
    return np.concatenate([x.reshape(-1, 16).T for x in idx]).astype(np.uint16)


def runs(offs, k):
    lists = np.stack([offs[16 * r : 16 * r + 16].T.reshape(-1) for r in range(8)]).astype(np.int64)
    return lists[np.arange(k) % 512 // 64]


def pack_weight(w):
    k, n = w.shape
    w = f64(np.asarray(w, np.float32).astype(ml_dtypes.bfloat16)).reshape(k // 32, 32, n)
    amax = np.abs(w).max(1)
    byte = np.clip(np.where(amax > 0, np.frexp(amax)[1] - 1 + 127 - 7, 1), 1, 254)
    scaled = (w * np.exp2(127.0 - byte)[:, None, :]).reshape(k, n).astype(np.float32)
    words = np.ascontiguousarray(scaled.reshape(k // 512, 128, 4, n).transpose(0, 1, 3, 2)).astype(ml_dtypes.float8_e4m3fn).view(np.uint8)
    return words, np.ascontiguousarray(byte.astype(np.uint8).reshape(k // 512, 16, n))


def unpack_weight(words, scales):
    g, p, n, _ = words.shape
    vals = np.ascontiguousarray(words).view(ml_dtypes.float8_e4m3fn).astype(np.float64) * np.repeat(np.exp2(scales.astype(np.float64) - 127.0), 8, axis=1)[..., None]
    return vals.transpose(0, 1, 3, 2).reshape(g * 512, n)


def sigmoid(v):
    return 1.0 / (1.0 + np.exp(-np.maximum(v, -700.0)))


K, T, S, H, G = 512, 2048, 256, 512, 2048


def setup_inputs():
    n = np.random.standard_normal
    s = mx_kscale(K)[:, None]
    packed_xT = pack_weight(n((K, T)) * s)
    packed_dT = pack_weight(n((K, G)) / s)
    return {
        "x_words": packed_xT[0],
        "x_scales": packed_xT[1],
        "w1": (n((K, H)) / np.sqrt(K) / s).astype(np.float32),
        "tau": np.random.uniform(0.2, 0.6, (H, 1)).astype(np.float32),
        "tau2": np.random.uniform(0.6, 1.0, (H, 1)).astype(np.float32),
        "gs": (np.random.uniform(0.5, 1.5, (K, 1)) * s).astype(np.float32),
        "d_words": packed_dT[0],
        "d_scales": packed_dT[1],
        "sl": np.random.uniform(1.5, 2.5, (H, 1)).astype(np.float32),
        "lo": np.random.uniform(-1.2, -0.4, (H, 1)).astype(np.float32),
        "hi": np.random.uniform(0.4, 1.2, (H, 1)).astype(np.float32),
        "offs": striped(np.random.permutation(T)[:S]),
        "n1": striped(np.random.permutation(S)),
        "n2": striped(np.random.permutation(S)),
        "k1": striped8(np.random.randint(0, G, (8, H))),
        "n3": striped8(np.stack([np.random.permutation(S) for _ in range(8)])),
    }


def reference(x_words, x_scales, w1, tau, tau2, gs, d_words, d_scales, sl, lo, hi, offs, n1, n2, k1, n3):
    d_k1 = unpack_weight(d_words, d_scales)[np.arange(K)[:, None], runs(k1, K)]
    xq = unpack_weight(x_words, x_scales)[:, unstriped(offs)]
    y = mxq(f64(w1), 0, "e4m3").T @ xq
    top = y.max(axis=1, keepdims=True)
    ea = np.exp(f64(tau) * (y[:, unstriped(n1)] - top))
    ea2 = np.exp(f64(tau2) * (y[:, unstriped(n2)] - top))
    z = f64(gs) * (3.0 * (ea - ea2))
    h = 0.0625 * ((d_k1.T @ mxq(z, 0, "e4m3")))
    sg = sigmoid(f64(sl) * (h[np.arange(H)[:, None], runs(n3, H)] - f64(lo)))
    sg2 = sigmoid(f64(sl) * (h[np.arange(H)[:, None], runs(n3, H)] - f64(hi)))
    return h * (sg - sg2)

@@ -1,0 +1,247 @@
+from contextlib import ExitStack
+
+import concourse.mybir as mybir
+
+F32 = mybir.dt.float32
+BF16 = mybir.dt.bfloat16
+I32 = mybir.dt.int32
+U32 = mybir.dt.uint32
+U16 = mybir.dt.uint16
+U8 = mybir.dt.uint8
+FP8X4 = mybir.dt.float8_e4m3fn_x4
+ALU = mybir.AluOpType
+ACT = mybir.ActivationFunctionType
+
+P = 128
+PACK = 4
+K, T, S, H, G = 512, 2048, 256, 512, 2048
+HALF = S // 2
+PER_COL = 16
+FLOPS = 2 * K * H * S + 2 * K * H * S
+
+
+def tile_picked_denseetwebd_none_p_kernel(
+    tc, x_words, x_scales, w1, tau, tau2, gs, d_words, d_scales, sl, lo, hi, offs, n1, n2, k1, n3, out
+):
+    nc = tc.nc
+    with ExitStack() as ctx:
+        keep = ctx.enter_context(tc.tile_pool(name="keep", bufs=1))
+        psum = ctx.enter_context(tc.psum_pool(name="psum", bufs=1))
+
+        def sb(name, shape, dtype, tag=None):
+            return keep.tile(shape, dtype, name=name, tag=tag or name, align_bytes=64)
+
+        def as_words(packed):
+            return packed[0].rearrange("p n r -> p (n r)").bitcast(I32)
+
+        def load_list(name, src):
+            tile = keep.tile(list(src.shape), U16, name=name)
+            nc.sync.dma_start(tile[:], src)
+            return tile
+
+        def load_rows(name, src):
+            tile = sb(name, [P, PACK], F32)
+            nc.sync.dma_start(tile[:], src.rearrange("(p t) o -> p (t o)", t=PACK))
+            return tile
+
+        x_scale_table = sb("x_scale_table", [P, T], U8)
+        d_scale_table = sb("d_scale_table", [P, G], U8)
+        d_scale_plane = sb("d_scale_plane", [P, H], U8)
+        nc.vector.memset(x_scale_table[:].bitcast(I32), 0)
+        nc.vector.memset(d_scale_table[:].bitcast(I32), 0)
+        nc.vector.memset(d_scale_plane[:].bitcast(I32), 0)
+
+        offs_sb = load_list("offs_sb", offs)
+        k1_sb = load_list("k1_sb", k1)
+        w_raw = sb("w_raw", [P, PACK, H], F32)
+        nc.sync.dma_start(w_raw[:], w1.rearrange("(p j) c -> p j c", j=PACK))
+        n3_sb = load_list("n3_sb", n3)
+        for q in range(4):
+            nc.sync.dma_start(
+                x_scale_table[32 * q + 4 : 32 * q + 8, :].bitcast(I32), x_scales[0, 4 * q : 4 * q + 4, :].bitcast(I32)
+            )
+        nc.sync.dma_start(d_scale_table[0:P:8, :].bitcast(I32), d_scales[0].bitcast(I32))
+        x_table = sb("x_table", [P, T], I32)
+        nc.sync.dma_start(x_table[:], as_words(x_words))
+        tau2_sb = load_rows("tau2_sb", tau2)
+        tau_sb = load_rows("tau_sb", tau)
+        n2_sb = load_list("n2_sb", n2)
+        n1_sb = load_list("n1_sb", n1)
+        sl_sb = load_rows("sl_sb", sl)
+        gs_sb = load_rows("gs_sb", gs)
+        d_table = sb("d_table", [P, G], I32)
+        nc.sync.dma_start(d_table[:], as_words(d_words))
+        lo_sb = load_rows("lo_sb", lo)
+        hi_sb = load_rows("hi_sb", hi)
+
+        y = [sb("y%d" % t, [P, 2 * S if t < 2 else S], F32) for t in range(PACK)]
+        h = [sb("h%d" % t, [P, 2 * S if t < 3 else S], F32) for t in range(PACK)]
+        for window in y[:2] + h[:3]:
+            nc.vector.memset(window[:, S : 2 * S], 0.0)
+
+        w_grouped = sb("w_grouped", [P, PACK, P, PACK], BF16)
+        w_src = w_raw[:].rearrange("p j (m t) -> p m t j", t=PACK)
+        w_dst = w_grouped[:].rearrange("p t m j -> p m t j")
+        split = 64
+        nc.scalar.activation(w_dst[:, split:P], w_src[:, split:P], ACT.Copy)
+        nc.vector.tensor_copy(w_dst[:, 0:split], w_src[:, 0:split])
+        x_scale = sb("x_scale", [P, S], U8)
+        nc.vector.tensor_copy(x_scale[:], x_scale_table[:].indirect(offs_sb[:]))
+        w_codes = sb("w_codes", [P, PACK, P], U32)
+        w_scale = sb("w_scale", [P, PACK, P], U8)
+        for t in range(PACK):
+            nc.vector.quantize_mx(
+                out=w_codes[:, t, :].bitcast(FP8X4),
+                scales=w_scale[:, t, :],
+                in_=w_grouped[:, t].rearrange("p m j -> p (m j)"),
+            )
+
+        d_scale_picked0 = sb("d_scale_picked0", [P, H // 2], U8)
+        nc.vector.tensor_copy(d_scale_picked0[:], d_scale_table[:].indirect(k1_sb[:, 0:16]))
+
+        neg_tau = sb("neg_tau", [P, PACK, 2], F32)
+        nc.scalar.activation(neg_tau[:, :, 0], tau_sb[:], ACT.Copy, scale=-1.0)
+        nc.scalar.activation(neg_tau[:, :, 1], tau2_sb[:], ACT.Copy, scale=-1.0)
+
+        x_codes = sb("x_codes", [P, S], U32)
+        nc.vector.tensor_copy(x_codes[:], x_table[:].bitcast(U32).indirect(offs_sb[:]))
+
+        y_bank = [psum.tile([P, S], F32, name="y_bank%d" % t) for t in range(PACK)]
+        for t in range(PACK):
+            nc.tensor.matmul_mx(
+                out=y_bank[t][:],
+                lhsT=w_codes[:, t, :].bitcast(FP8X4),
+                lhsT_scale=w_scale[:, t, :],
+                rhs=x_codes[:].bitcast(FP8X4),
+                rhs_scale=x_scale[4:P, :],
+                start=True,
+                stop=True,
+            )
+
+        exp_bias = sb("exp_bias", [P, PACK, 2], F32)
+        for tiles in ((0,), (1,), (2, 3)):
+            top = sb("top%d" % tiles[0], [P, len(tiles), 1], F32)
+            for i, t in enumerate(tiles):
+                nc.vector.tensor_scalar(y[t][:, 0:S], y_bank[t][:], 1.0, None, ALU.mult, ALU.max, accum_out=top[:, i, :])
+            rows = slice(tiles[0], tiles[-1] + 1)
+            nc.vector.tensor_tensor(
+                exp_bias[:, rows, :], neg_tau[:, rows, :], top[:].to_broadcast([P, len(tiles), 2]), ALU.mult
+            )
+
+        d_scale_picked1 = sb("d_scale_picked1", [P, H // 2], U8, tag="x_table")
+        nc.vector.tensor_copy(d_scale_picked1[:], d_scale_table[:].indirect(k1_sb[:, 16:32]))
+        d_scale_dealt = sb("d_scale_dealt", [P, PACK, P], U8, tag="top0")
+        for b, picked in enumerate((d_scale_picked0, d_scale_picked1)):
+            nc.vector.tensor_copy(
+                d_scale_dealt[:, :, b * 64 : (b + 1) * 64].rearrange("p t m -> p m t"),
+                picked[:].rearrange("p (m t) -> p m t", t=PACK),
+            )
+        for q in range(4):
+            nc.sync.dma_start(
+                d_scale_plane[32 * q : 32 * q + 4, :].bitcast(I32),
+                d_scale_dealt[32 * q : 32 * q + 32 : 8].rearrange("p t m -> p (t m)").bitcast(I32),
+            )
+
+        gs3 = sb("gs3", [P, PACK], F32)
+        nc.gpsimd.tensor_scalar(gs3[:], gs_sb[:], 3.0, 0.0, ALU.mult, ALU.add)
+        neg_sl = sb("neg_sl", [P, PACK], F32)
+        nc.scalar.activation(neg_sl[:], sl_sb[:], ACT.Copy, scale=-1.0)
+
+        d_picked = sb("d_picked", [P, H], U32)
+        d_codes = sb("d_codes", [P, PACK, P], U32)
+        for b in range(2):
+            nc.vector.tensor_copy(
+                d_picked[:, b * 256 : (b + 1) * 256],
+                d_table[:].bitcast(U32).indirect(k1_sb[:, b * 16 : (b + 1) * 16]),
+            )
+        nc.vector.tensor_copy(
+            d_codes[:].rearrange("p t m -> p m t"), d_picked[:].rearrange("p (m t) -> p m t", t=PACK)
+        )
+        lo_bias = sb("lo_bias", [P, PACK], F32)
+        hi_bias = sb("hi_bias", [P, PACK], F32)
+        nc.vector.tensor_tensor(lo_bias[:], lo_sb[:], neg_sl[:], ALU.mult)
+        nc.vector.tensor_tensor(hi_bias[:], hi_sb[:], neg_sl[:], ALU.mult)
+
+        h_bank = [psum.tile([P, S], F32, name="h_bank%d" % t) for t in range(PACK)]
+        halves = [slice(a * HALF, (a + 1) * HALF) for a in range(2)]
+
+        whole = slice(0, S)
+
+        def entries(tile, cols):
+            return tile[:, cols.start // PER_COL : cols.stop // PER_COL]
+
+        z_planes = sb("z_planes", [P, PACK, S], BF16)
+        ea2g = sb("ea2g", [P, PACK, S], F32, tag="d_picked")
+
+        def z_plane(t, cols, ea, ea2):
+            nc.vector.tensor_scalar(ea2g[:, t, cols], ea2[:, cols], gs3[:, t : t + 1], None, ALU.mult)
+            nc.vector.scalar_tensor_tensor(
+                z_planes[:, t, cols], ea[:, cols], gs3[:, t : t + 1], ea2g[:, t, cols], ALU.mult, ALU.subtract
+            )
+
+        def second_product(a):
+            grouped = sb("z_grouped%d" % a, [P, HALF, PACK], BF16)
+            nc.vector.tensor_copy(grouped[:], z_planes[:, :, halves[a]].rearrange("p t j -> p j t"))
+            codes = sb("z_codes%d" % a, [P, HALF], U32)
+            scale = sb("z_scale%d" % a, [P, HALF], U8)
+            nc.vector.quantize_mx(
+                out=codes[:].bitcast(FP8X4), scales=scale[:], in_=grouped[:].rearrange("p j t -> p (j t)")
+            )
+            for t in range(PACK):
+                nc.tensor.matmul_mx(
+                    out=h_bank[t][:, halves[a]],
+                    lhsT=d_codes[:, t, :].bitcast(FP8X4),
+                    lhsT_scale=d_scale_plane[:, t * P : (t + 1) * P],
+                    rhs=codes[:].bitcast(FP8X4),
+                    rhs_scale=scale[:],
+                    start=True,
+                    stop=True,
+                )
+
+        last = PACK - 1
+        ea = [sb("ea%d" % t, [P, S], F32) for t in range(PACK)]
+        ea2 = [sb("ea2_%d" % t, [P, S], F32) for t in range(PACK)]
+
+        def exps(t, cols):
+            nc.scalar.activation(
+                ea2[t][:, cols], y[t][:].indirect(entries(n2_sb, cols)), ACT.Exp,
+                bias=exp_bias[:, t, 1:2], scale=tau2_sb[:, t : t + 1],
+            )
+            nc.scalar.activation(
+                ea[t][:, cols], y[t][:].indirect(entries(n1_sb, cols)), ACT.Exp,
+                bias=exp_bias[:, t, 0:1], scale=tau_sb[:, t : t + 1],
+            )
+            z_plane(t, cols, ea[t], ea2[t])
+
+        for t in (0, 1):
+            exps(t, whole)
+        for a in range(2):
+            for t in (2, 3):
+                exps(t, halves[a])
+            second_product(a)
+
+        out_rows = out.rearrange("(p t) j -> p t j", t=PACK)
+        for t in range(PACK):
+            nc.vector.tensor_scalar(h[t][:, 0:S], h_bank[t][:], 0.0625, None, ALU.mult)
+
+        def finish(t, cols, sg, sg2):
+            width = cols.stop - cols.start
+            band = sb("band%d_%d" % (t, cols.start), [P, width], F32)
+            res = sb("res%d_%d" % (t, cols.start), [P, width], F32)
+            nc.vector.tensor_tensor(band[:], sg[:, cols], sg2[:, cols], ALU.subtract)
+            nc.vector.tensor_tensor(res[:], band[:], h[t][:, cols], ALU.mult)
+            nc.sync.dma_start(out_rows[:, t, cols], res[:])
+
+        for t in range(PACK):
+            sg = sb("sg%d" % t, [P, S], F32)
+            sg2 = sb("sg2_%d" % t, [P, S], F32)
+            for cols in (halves if t == last else [whole]):
+                nc.scalar.activation(
+                    sg[:, cols], h[t][:].indirect(entries(n3_sb, cols)), ACT.Sigmoid,
+                    bias=lo_bias[:, t : t + 1], scale=sl_sb[:, t : t + 1],
+                )
+                nc.scalar.activation(
+                    sg2[:, cols], h[t][:].indirect(entries(n3_sb, cols)), ACT.Sigmoid,
+                    bias=hi_bias[:, t : t + 1], scale=sl_sb[:, t : t + 1],
+                )
+                finish(t, cols, sg, sg2)

@@ -54,13 +54,13 @@ def tile_picked_denseetwebd_none_p_kernel(
         offs_sb = load_list("offs_sb", offs)
         k1_sb = load_list("k1_sb", k1)
         w_raw = sb("w_raw", [P, PACK, H], F32)
-        nc.sync.dma_start(w_raw[:], w1.rearrange("(p j) c -> p j c", j=PACK))
+        w_rows = w1.rearrange("(p j) c -> p j c", j=PACK)
+        nc.sync.dma_start(w_raw[:, 0:2, :], w_rows[:, 0:2, :])
         n3_sb = load_list("n3_sb", n3)
-        for q in range(4):
-            nc.sync.dma_start(
-                x_scale_table[32 * q + 4 : 32 * q + 8, :].bitcast(I32), x_scales[0, 4 * q : 4 * q + 4, :].bitcast(I32)
-            )
+        for r in range(4):
+            nc.sync.dma_start(x_scale_table[4 + r : P : 32, :].bitcast(I32), x_scales[0, r:16:4, :].bitcast(I32))
         nc.sync.dma_start(d_scale_table[0:P:8, :].bitcast(I32), d_scales[0].bitcast(I32))
+        nc.sync.dma_start(w_raw[:, 2:4, :], w_rows[:, 2:4, :])
         x_table = sb("x_table", [P, T], I32)
         nc.sync.dma_start(x_table[:], as_words(x_words))
         tau2_sb = load_rows("tau2_sb", tau2)
@@ -96,8 +96,20 @@ def tile_picked_denseetwebd_none_p_kernel(
                 in_=w_grouped[:, t].rearrange("p m j -> p (m j)"),
             )
 
-        d_scale_picked0 = sb("d_scale_picked0", [P, H // 2], U8)
-        nc.vector.tensor_copy(d_scale_picked0[:], d_scale_table[:].indirect(k1_sb[:, 0:16]))
+        d_scale_picked = sb("d_scale_picked", [P, H], U8)
+        for b in range(2):
+            nc.vector.tensor_copy(
+                d_scale_picked[:, b * 256 : (b + 1) * 256], d_scale_table[:].indirect(k1_sb[:, b * 16 : (b + 1) * 16])
+            )
+        d_scale_dealt = sb("d_scale_dealt", [P, H], U8)
+        nc.vector.tensor_copy(
+            d_scale_dealt[:].rearrange("p (t m) -> p m t", t=PACK),
+            d_scale_picked[:].rearrange("p (m t) -> p m t", t=PACK),
+        )
+        for r in range(4):
+            nc.sync.dma_start(
+                d_scale_plane[r:P:32, :].bitcast(I32), d_scale_dealt[8 * r : P : 32, :].bitcast(I32)
+            )
 
         neg_tau = sb("neg_tau", [P, PACK, 2], F32)
         nc.scalar.activation(neg_tau[:, :, 0], tau_sb[:], ACT.Copy, scale=-1.0)
@@ -119,28 +131,24 @@ def tile_picked_denseetwebd_none_p_kernel(
             )
 
         exp_bias = sb("exp_bias", [P, PACK, 2], F32)
-        for tiles in ((0,), (1,), (2, 3)):
-            top = sb("top%d" % tiles[0], [P, len(tiles), 1], F32)
-            for i, t in enumerate(tiles):
-                nc.vector.tensor_scalar(y[t][:, 0:S], y_bank[t][:], 1.0, None, ALU.mult, ALU.max, accum_out=top[:, i, :])
-            rows = slice(tiles[0], tiles[-1] + 1)
+        top0 = sb("top0", [P, 1, 1], F32)
+        top = sb("top", [P, PACK - 1, 1], F32)
+
+        def y_out(t, top_col):
+            nc.vector.tensor_scalar(y[t][:, 0:S], y_bank[t][:], 1.0, None, ALU.mult, ALU.max, accum_out=top_col)
+
+        def biases(t0, t1, tops):
             nc.vector.tensor_tensor(
-                exp_bias[:, rows, :], neg_tau[:, rows, :], top[:].to_broadcast([P, len(tiles), 2]), ALU.mult
+                exp_bias[:, t0:t1, :], neg_tau[:, t0:t1, :], tops.to_broadcast([P, t1 - t0, 2]), ALU.mult
             )
 
-        d_scale_picked1 = sb("d_scale_picked1", [P, H // 2], U8, tag="x_table")
-        nc.vector.tensor_copy(d_scale_picked1[:], d_scale_table[:].indirect(k1_sb[:, 16:32]))
-        d_scale_dealt = sb("d_scale_dealt", [P, PACK, P], U8, tag="top0")
-        for b, picked in enumerate((d_scale_picked0, d_scale_picked1)):
-            nc.vector.tensor_copy(
-                d_scale_dealt[:, :, b * 64 : (b + 1) * 64].rearrange("p t m -> p m t"),
-                picked[:].rearrange("p (m t) -> p m t", t=PACK),
-            )
-        for q in range(4):
-            nc.sync.dma_start(
-                d_scale_plane[32 * q : 32 * q + 4, :].bitcast(I32),
-                d_scale_dealt[32 * q : 32 * q + 32 : 8].rearrange("p t m -> p (t m)").bitcast(I32),
-            )
+        y_out(0, top0[:, 0, :])
+        biases(0, 1, top0[:])
+        y_out(1, top[:, 0, :])
+        y_out(2, top[:, 1, :])
+        biases(1, 2, top[:, 0:1, :])
+        y_out(3, top[:, 2, :])
+        biases(2, 4, top[:, 1:3, :])
 
         gs3 = sb("gs3", [P, PACK], F32)
         nc.gpsimd.tensor_scalar(gs3[:], gs_sb[:], 3.0, 0.0, ALU.mult, ALU.add)
@@ -154,50 +162,31 @@ def tile_picked_denseetwebd_none_p_kernel(
                 d_picked[:, b * 256 : (b + 1) * 256],
                 d_table[:].bitcast(U32).indirect(k1_sb[:, b * 16 : (b + 1) * 16]),
             )
-        nc.vector.tensor_copy(
-            d_codes[:].rearrange("p t m -> p m t"), d_picked[:].rearrange("p (m t) -> p m t", t=PACK)
-        )
         lo_bias = sb("lo_bias", [P, PACK], F32)
         hi_bias = sb("hi_bias", [P, PACK], F32)
         nc.vector.tensor_tensor(lo_bias[:], lo_sb[:], neg_sl[:], ALU.mult)
         nc.vector.tensor_tensor(hi_bias[:], hi_sb[:], neg_sl[:], ALU.mult)
 
+        def deal_words(t0, t1):
+            nc.vector.tensor_copy(
+                d_codes[:, t0:t1, :].rearrange("p t m -> p m t"),
+                d_picked[:].rearrange("p (m t) -> p m t", t=PACK)[:, :, t0:t1],
+            )
+
+        deal_words(0, 1)
+
         h_bank = [psum.tile([P, S], F32, name="h_bank%d" % t) for t in range(PACK)]
         halves = [slice(a * HALF, (a + 1) * HALF) for a in range(2)]
-
         whole = slice(0, S)
 
         def entries(tile, cols):
             return tile[:, cols.start // PER_COL : cols.stop // PER_COL]
 
         z_planes = sb("z_planes", [P, PACK, S], BF16)
-        ea2g = sb("ea2g", [P, PACK, S], F32, tag="d_picked")
-
-        def z_plane(t, cols, ea, ea2):
-            nc.vector.tensor_scalar(ea2g[:, t, cols], ea2[:, cols], gs3[:, t : t + 1], None, ALU.mult)
-            nc.vector.scalar_tensor_tensor(
-                z_planes[:, t, cols], ea[:, cols], gs3[:, t : t + 1], ea2g[:, t, cols], ALU.mult, ALU.subtract
-            )
-
-        def second_product(a):
-            grouped = sb("z_grouped%d" % a, [P, HALF, PACK], BF16)
-            nc.vector.tensor_copy(grouped[:], z_planes[:, :, halves[a]].rearrange("p t j -> p j t"))
-            codes = sb("z_codes%d" % a, [P, HALF], U32)
-            scale = sb("z_scale%d" % a, [P, HALF], U8)
-            nc.vector.quantize_mx(
-                out=codes[:].bitcast(FP8X4), scales=scale[:], in_=grouped[:].rearrange("p j t -> p (j t)")
-            )
-            for t in range(PACK):
-                nc.tensor.matmul_mx(
-                    out=h_bank[t][:, halves[a]],
-                    lhsT=d_codes[:, t, :].bitcast(FP8X4),
-                    lhsT_scale=d_scale_plane[:, t * P : (t + 1) * P],
-                    rhs=codes[:].bitcast(FP8X4),
-                    rhs_scale=scale[:],
-                    start=True,
-                    stop=True,
-                )
-
+        ea2g = sb("ea2g", [P, PACK, S], F32, tag="d_table")
+        z_grouped = sb("z_grouped", [P, S, PACK], BF16)
+        z_codes = sb("z_codes", [P, S], U32)
+        z_scale = sb("z_scale", [P, S], U8)
         last = PACK - 1
         ea = [sb("ea%d" % t, [P, S], F32) for t in range(PACK)]
         ea2 = [sb("ea2_%d" % t, [P, S], F32) for t in range(PACK)]
@@ -211,14 +200,64 @@ def tile_picked_denseetwebd_none_p_kernel(
                 ea[t][:, cols], y[t][:].indirect(entries(n1_sb, cols)), ACT.Exp,
                 bias=exp_bias[:, t, 0:1], scale=tau_sb[:, t : t + 1],
             )
-            z_plane(t, cols, ea[t], ea2[t])
 
-        for t in (0, 1):
-            exps(t, whole)
-        for a in range(2):
-            for t in (2, 3):
-                exps(t, halves[a])
-            second_product(a)
+        def weigh(t, cols):
+            nc.vector.tensor_scalar(ea2g[:, t, cols], ea2[t][:, cols], gs3[:, t : t + 1], None, ALU.mult)
+
+        def z_plane(t, cols):
+            nc.vector.scalar_tensor_tensor(
+                z_planes[:, t, cols], ea[t][:, cols], gs3[:, t : t + 1], ea2g[:, t, cols], ALU.mult, ALU.subtract
+            )
+
+        def interleave(cols):
+            nc.vector.tensor_copy(z_grouped[:, cols, :], z_planes[:, :, cols].rearrange("p t j -> p j t"))
+
+        def quantise(cols):
+            nc.vector.quantize_mx(
+                out=z_codes[:, cols].bitcast(FP8X4),
+                scales=z_scale[:, cols],
+                in_=z_grouped[:, cols, :].rearrange("p j t -> p (j t)"),
+            )
+
+        def second_product(t, cols):
+            nc.tensor.matmul_mx(
+                out=h_bank[t][:, cols],
+                lhsT=d_codes[:, t, :].bitcast(FP8X4),
+                lhsT_scale=d_scale_plane[:, t * P : (t + 1) * P],
+                rhs=z_codes[:, cols].bitcast(FP8X4),
+                rhs_scale=z_scale[:, cols],
+                start=True,
+                stop=True,
+            )
+
+        first, second = halves
+        exps(0, whole)
+        exps(1, whole)
+        exps(2, first)
+        exps(3, first)
+        exps(2, second)
+        exps(3, second)
+        weigh(0, whole)
+        weigh(1, whole)
+        z_plane(0, whole)
+        weigh(2, first)
+        z_plane(1, whole)
+        weigh(3, first)
+        z_plane(2, first)
+        z_plane(3, first)
+        weigh(2, second)
+        interleave(first)
+        z_plane(2, second)
+        quantise(first)
+        second_product(0, first)
+        weigh(3, second)
+        z_plane(3, second)
+        interleave(second)
+        quantise(second)
+        second_product(0, second)
+        deal_words(1, PACK)
+        for t in range(1, PACK):
+            second_product(t, whole)
 
         out_rows = out.rearrange("(p t) j -> p t j", t=PACK)
         for t in range(PACK):

@@ -56,7 +56,6 @@ def tile_picked_denseetwebd_none_p_kernel(
         w_raw = sb("w_raw", [P, PACK, H], F32)
         w_rows = w1.rearrange("(p j) c -> p j c", j=PACK)
         nc.sync.dma_start(w_raw[:, 0:2, :], w_rows[:, 0:2, :])
-        n3_sb = load_list("n3_sb", n3)
         for r in range(4):
             nc.sync.dma_start(x_scale_table[4 + r : P : 32, :].bitcast(I32), x_scales[0, r:16:4, :].bitcast(I32))
         nc.sync.dma_start(d_scale_table[0:P:8, :].bitcast(I32), d_scales[0].bitcast(I32))
@@ -67,10 +66,11 @@ def tile_picked_denseetwebd_none_p_kernel(
         tau_sb = load_rows("tau_sb", tau)
         n2_sb = load_list("n2_sb", n2)
         n1_sb = load_list("n1_sb", n1)
-        sl_sb = load_rows("sl_sb", sl)
         gs_sb = load_rows("gs_sb", gs)
         d_table = sb("d_table", [P, G], I32)
         nc.sync.dma_start(d_table[:], as_words(d_words))
+        n3_sb = load_list("n3_sb", n3)
+        sl_sb = load_rows("sl_sb", sl)
         lo_sb = load_rows("lo_sb", lo)
         hi_sb = load_rows("hi_sb", hi)
 
@@ -115,45 +115,63 @@ def tile_picked_denseetwebd_none_p_kernel(
         nc.scalar.activation(neg_tau[:, :, 0], tau_sb[:], ACT.Copy, scale=-1.0)
         nc.scalar.activation(neg_tau[:, :, 1], tau2_sb[:], ACT.Copy, scale=-1.0)
 
-        x_codes = sb("x_codes", [P, S], U32)
-        nc.vector.tensor_copy(x_codes[:], x_table[:].bitcast(U32).indirect(offs_sb[:]))
+        halves = [slice(a * HALF, (a + 1) * HALF) for a in range(2)]
+        first, second = halves
+        whole = slice(0, S)
 
-        y_bank = [psum.tile([P, S], F32, name="y_bank%d" % t) for t in range(PACK)]
-        for t in range(PACK):
+        def entries(tile, cols):
+            return tile[:, cols.start // PER_COL : cols.stop // PER_COL]
+
+        x_codes = sb("x_codes", [P, S], U32)
+        for cols in halves:
+            nc.vector.tensor_copy(x_codes[:, cols], x_table[:].bitcast(U32).indirect(entries(offs_sb, cols)))
+
+        def first_product(bank, t, cols):
             nc.tensor.matmul_mx(
-                out=y_bank[t][:],
+                out=bank,
                 lhsT=w_codes[:, t, :].bitcast(FP8X4),
                 lhsT_scale=w_scale[:, t, :],
-                rhs=x_codes[:].bitcast(FP8X4),
-                rhs_scale=x_scale[4:P, :],
+                rhs=x_codes[:, cols].bitcast(FP8X4),
+                rhs_scale=x_scale[4:P, cols],
                 start=True,
                 stop=True,
             )
 
-        exp_bias = sb("exp_bias", [P, PACK, 2], F32)
-        top0 = sb("top0", [P, 1, 1], F32)
+        y_early = psum.tile([P, HALF], F32, name="y_early", tag="early")
+        y_bank = [psum.tile([P, S], F32, name="y_bank%d" % t, tag="bank%d" % t) for t in range(PACK)]
+        first_product(y_early[:], 0, first)
+        first_product(y_bank[0][:, second], 0, second)
+        for t in range(1, PACK):
+            first_product(y_bank[t][:], t, whole)
+
+        bias0 = sb("bias0", [P, 2], F32)
+        bias_rest = sb("bias_rest", [P, PACK - 1, 2], F32)
+        exp_bias = [bias0[:]] + [bias_rest[:, t, :] for t in range(PACK - 1)]
+        top_early = sb("top_early", [P, 1], F32)
+        top0 = sb("top0", [P, 1], F32)
         top = sb("top", [P, PACK - 1, 1], F32)
 
         def y_out(t, top_col):
             nc.vector.tensor_scalar(y[t][:, 0:S], y_bank[t][:], 1.0, None, ALU.mult, ALU.max, accum_out=top_col)
 
-        def biases(t0, t1, tops):
-            nc.vector.tensor_tensor(
-                exp_bias[:, t0:t1, :], neg_tau[:, t0:t1, :], tops.to_broadcast([P, t1 - t0, 2]), ALU.mult
+        def biases(engine, dst, t0, t1, tops):
+            engine.tensor_tensor(
+                dst, neg_tau[:, t0:t1, :], tops.to_broadcast([P, t1 - t0, 2]), ALU.mult
             )
 
-        y_out(0, top0[:, 0, :])
-        biases(0, 1, top0[:])
+        nc.vector.tensor_scalar(y[0][:, first], y_early[:], 1.0, None, ALU.mult, ALU.max, accum_out=top_early[:])
+        nc.vector.tensor_scalar(
+            y[0][:, second], y_bank[0][:, second], 1.0, top_early[:], ALU.mult, ALU.max, accum_out=top0[:]
+        )
+        nc.scalar.activation(bias0[:], neg_tau[:, 0, :], ACT.Copy, scale=top0[:])
         y_out(1, top[:, 0, :])
         y_out(2, top[:, 1, :])
-        biases(1, 2, top[:, 0:1, :])
+        biases(nc.gpsimd, bias_rest[:, 0:1, :], 1, 2, top[:, 0:1, :])
         y_out(3, top[:, 2, :])
-        biases(2, 4, top[:, 1:3, :])
+        biases(nc.gpsimd, bias_rest[:, 1:3, :], 2, 4, top[:, 1:3, :])
 
         gs3 = sb("gs3", [P, PACK], F32)
         nc.gpsimd.tensor_scalar(gs3[:], gs_sb[:], 3.0, 0.0, ALU.mult, ALU.add)
-        neg_sl = sb("neg_sl", [P, PACK], F32)
-        nc.scalar.activation(neg_sl[:], sl_sb[:], ACT.Copy, scale=-1.0)
 
         d_picked = sb("d_picked", [P, H], U32)
         d_codes = sb("d_codes", [P, PACK, P], U32)
@@ -164,8 +182,6 @@ def tile_picked_denseetwebd_none_p_kernel(
             )
         lo_bias = sb("lo_bias", [P, PACK], F32)
         hi_bias = sb("hi_bias", [P, PACK], F32)
-        nc.vector.tensor_tensor(lo_bias[:], lo_sb[:], neg_sl[:], ALU.mult)
-        nc.vector.tensor_tensor(hi_bias[:], hi_sb[:], neg_sl[:], ALU.mult)
 
         def deal_words(t0, t1):
             nc.vector.tensor_copy(
@@ -175,12 +191,7 @@ def tile_picked_denseetwebd_none_p_kernel(
 
         deal_words(0, 1)
 
-        h_bank = [psum.tile([P, S], F32, name="h_bank%d" % t) for t in range(PACK)]
-        halves = [slice(a * HALF, (a + 1) * HALF) for a in range(2)]
-        whole = slice(0, S)
-
-        def entries(tile, cols):
-            return tile[:, cols.start // PER_COL : cols.stop // PER_COL]
+        h_bank = [psum.tile([P, S], F32, name="h_bank%d" % t, tag="bank0" if t == 0 else "h_bank%d" % t) for t in range(PACK)]
 
         z_planes = sb("z_planes", [P, PACK, S], BF16)
         ea2g = sb("ea2g", [P, PACK, S], F32, tag="d_table")
@@ -194,11 +205,11 @@ def tile_picked_denseetwebd_none_p_kernel(
         def exps(t, cols):
             nc.scalar.activation(
                 ea2[t][:, cols], y[t][:].indirect(entries(n2_sb, cols)), ACT.Exp,
-                bias=exp_bias[:, t, 1:2], scale=tau2_sb[:, t : t + 1],
+                bias=exp_bias[t][:, 1:2], scale=tau2_sb[:, t : t + 1],
             )
             nc.scalar.activation(
                 ea[t][:, cols], y[t][:].indirect(entries(n1_sb, cols)), ACT.Exp,
-                bias=exp_bias[:, t, 0:1], scale=tau_sb[:, t : t + 1],
+                bias=exp_bias[t][:, 0:1], scale=tau_sb[:, t : t + 1],
             )
 
         def weigh(t, cols):
@@ -219,9 +230,9 @@ def tile_picked_denseetwebd_none_p_kernel(
                 in_=z_grouped[:, cols, :].rearrange("p j t -> p (j t)"),
             )
 
-        def second_product(t, cols):
+        def second_product(bank, t, cols):
             nc.tensor.matmul_mx(
-                out=h_bank[t][:, cols],
+                out=bank,
                 lhsT=d_codes[:, t, :].bitcast(FP8X4),
                 lhsT_scale=d_scale_plane[:, t * P : (t + 1) * P],
                 rhs=z_codes[:, cols].bitcast(FP8X4),
@@ -230,18 +241,22 @@ def tile_picked_denseetwebd_none_p_kernel(
                 stop=True,
             )
 
-        first, second = halves
+        def h_out(t, cols, bank):
+            nc.vector.tensor_scalar(h[t][:, cols], bank, 0.0625, None, ALU.mult)
+
+        third, fourth = slice(HALF, HALF + 64), slice(HALF + 64, S)
         exps(0, whole)
         exps(1, whole)
         exps(2, first)
         exps(3, first)
         exps(2, second)
-        exps(3, second)
-        weigh(0, whole)
-        weigh(1, whole)
-        z_plane(0, whole)
+        exps(3, third)
+        exps(3, fourth)
+        for t in (0, 1):
+            diff = sb("diff%d" % t, [P, S], F32)
+            nc.gpsimd.tensor_tensor(diff[:], ea[t][:], ea2[t][:], ALU.subtract)
+            nc.gpsimd.tensor_scalar(z_planes[:, t, :], diff[:], gs3[:, t : t + 1], 0.0, ALU.mult, ALU.add)
         weigh(2, first)
-        z_plane(1, whole)
         weigh(3, first)
         z_plane(2, first)
         z_plane(3, first)
@@ -249,19 +264,28 @@ def tile_picked_denseetwebd_none_p_kernel(
         interleave(first)
         z_plane(2, second)
         quantise(first)
-        second_product(0, first)
-        weigh(3, second)
-        z_plane(3, second)
-        interleave(second)
-        quantise(second)
-        second_product(0, second)
+        h_early = psum.tile([P, HALF], F32, name="h_early", tag="early")
+        second_product(h_early[:], 0, first)
+        weigh(3, third)
+        z_plane(3, third)
+        weigh(3, fourth)
+        interleave(third)
+        z_plane(3, fourth)
+        quantise(third)
+        interleave(fourth)
+        h_out(0, first, h_early[:])
+        quantise(fourth)
+        second_product(h_bank[0][:, second], 0, second)
+        nc.vector.scalar_tensor_tensor(lo_bias[:], lo_sb[:], -1.0, sl_sb[:], ALU.mult, ALU.mult)
+        nc.vector.scalar_tensor_tensor(hi_bias[:], hi_sb[:], -1.0, sl_sb[:], ALU.mult, ALU.mult)
         deal_words(1, PACK)
         for t in range(1, PACK):
-            second_product(t, whole)
+            second_product(h_bank[t][:], t, whole)
+        h_out(0, second, h_bank[0][:, second])
+        for t in range(1, PACK):
+            h_out(t, whole, h_bank[t][:])
 
         out_rows = out.rearrange("(p t) j -> p t j", t=PACK)
-        for t in range(PACK):
-            nc.vector.tensor_scalar(h[t][:, 0:S], h_bank[t][:], 0.0625, None, ALU.mult)
 
         def finish(t, cols, sg, sg2):
             width = cols.stop - cols.start

from contextlib import ExitStack

import concourse.mybir as mybir

F32 = mybir.dt.float32
BF16 = mybir.dt.bfloat16
I32 = mybir.dt.int32
U32 = mybir.dt.uint32
U16 = mybir.dt.uint16
U8 = mybir.dt.uint8
FP8X4 = mybir.dt.float8_e4m3fn_x4
ALU = mybir.AluOpType
ACT = mybir.ActivationFunctionType

P = 128
PACK = 4
K, T, S, H, G = 512, 2048, 256, 512, 2048
HALF = S // 2
PER_COL = 16
FLOPS = 2 * K * H * S + 2 * K * H * S


def tile_picked_denseetwebd_none_p_kernel(
    tc, x_words, x_scales, w1, tau, tau2, gs, d_words, d_scales, sl, lo, hi, offs, n1, n2, k1, n3, out
):
    nc = tc.nc
    with ExitStack() as ctx:
        keep = ctx.enter_context(tc.tile_pool(name="keep", bufs=1))
        psum = ctx.enter_context(tc.psum_pool(name="psum", bufs=1))

        def sb(name, shape, dtype, tag=None):
            return keep.tile(shape, dtype, name=name, tag=tag or name, align_bytes=64)

        def as_words(packed):
            return packed[0].rearrange("p n r -> p (n r)").bitcast(I32)

        def load_list(name, src):
            tile = keep.tile(list(src.shape), U16, name=name)
            nc.sync.dma_start(tile[:], src)
            return tile

        def load_rows(name, src):
            tile = sb(name, [P, PACK], F32)
            nc.sync.dma_start(tile[:], src.rearrange("(p t) o -> p (t o)", t=PACK))
            return tile

        x_scale_table = sb("x_scale_table", [P, T], U8)
        d_scale_table = sb("d_scale_table", [P, G], U8)
        d_scale_plane = sb("d_scale_plane", [P, H], U8)
        nc.vector.memset(x_scale_table[:].bitcast(I32), 0)
        nc.vector.memset(d_scale_table[:].bitcast(I32), 0)
        nc.vector.memset(d_scale_plane[:].bitcast(I32), 0)

        offs_sb = load_list("offs_sb", offs)
        k1_sb = load_list("k1_sb", k1)
        w_raw = sb("w_raw", [P, PACK, H], F32)
        w_rows = w1.rearrange("(p j) c -> p j c", j=PACK)
        nc.sync.dma_start(w_raw[:, 0:2, :], w_rows[:, 0:2, :])
        for r in range(4):
            nc.sync.dma_start(x_scale_table[4 + r : P : 32, :].bitcast(I32), x_scales[0, r:16:4, :].bitcast(I32))
        nc.sync.dma_start(d_scale_table[0:P:8, :].bitcast(I32), d_scales[0].bitcast(I32))
        nc.sync.dma_start(w_raw[:, 2:4, :], w_rows[:, 2:4, :])
        x_table = sb("x_table", [P, T], I32)
        nc.sync.dma_start(x_table[:], as_words(x_words))
        tau2_sb = load_rows("tau2_sb", tau2)
        tau_sb = load_rows("tau_sb", tau)
        n2_sb = load_list("n2_sb", n2)
        n1_sb = load_list("n1_sb", n1)
        gs_sb = load_rows("gs_sb", gs)
        d_table = sb("d_table", [P, G], I32)
        nc.sync.dma_start(d_table[:], as_words(d_words))
        n3_sb = load_list("n3_sb", n3)
        sl_sb = load_rows("sl_sb", sl)
        lo_sb = load_rows("lo_sb", lo)
        hi_sb = load_rows("hi_sb", hi)

        y = [sb("y%d" % t, [P, 2 * S if t < 2 else S], F32) for t in range(PACK)]
        h = [sb("h%d" % t, [P, 2 * S if t < 3 else S], F32) for t in range(PACK)]
        for window in y[:2] + h[:3]:
            nc.vector.memset(window[:, S : 2 * S], 0.0)

        w_grouped = sb("w_grouped", [P, PACK, P, PACK], BF16)
        w_src = w_raw[:].rearrange("p j (m t) -> p m t j", t=PACK)
        w_dst = w_grouped[:].rearrange("p t m j -> p m t j")
        split = 64
        nc.scalar.activation(w_dst[:, split:P], w_src[:, split:P], ACT.Copy)
        nc.vector.tensor_copy(w_dst[:, 0:split], w_src[:, 0:split])
        x_scale = sb("x_scale", [P, S], U8)
        nc.vector.tensor_copy(x_scale[:], x_scale_table[:].indirect(offs_sb[:]))
        w_codes = sb("w_codes", [P, PACK, P], U32)
        w_scale = sb("w_scale", [P, PACK, P], U8)
        for t in range(PACK):
            nc.vector.quantize_mx(
                out=w_codes[:, t, :].bitcast(FP8X4),
                scales=w_scale[:, t, :],
                in_=w_grouped[:, t].rearrange("p m j -> p (m j)"),
            )

        d_scale_picked = sb("d_scale_picked", [P, H], U8)
        for b in range(2):
            nc.vector.tensor_copy(
                d_scale_picked[:, b * 256 : (b + 1) * 256], d_scale_table[:].indirect(k1_sb[:, b * 16 : (b + 1) * 16])
            )
        d_scale_dealt = sb("d_scale_dealt", [P, H], U8)
        nc.vector.tensor_copy(
            d_scale_dealt[:].rearrange("p (t m) -> p m t", t=PACK),
            d_scale_picked[:].rearrange("p (m t) -> p m t", t=PACK),
        )
        for r in range(4):
            nc.sync.dma_start(
                d_scale_plane[r:P:32, :].bitcast(I32), d_scale_dealt[8 * r : P : 32, :].bitcast(I32)
            )

        neg_tau = sb("neg_tau", [P, PACK, 2], F32)
        nc.scalar.activation(neg_tau[:, :, 0], tau_sb[:], ACT.Copy, scale=-1.0)
        nc.scalar.activation(neg_tau[:, :, 1], tau2_sb[:], ACT.Copy, scale=-1.0)

        halves = [slice(a * HALF, (a + 1) * HALF) for a in range(2)]
        first, second = halves
        whole = slice(0, S)

        def entries(tile, cols):
            return tile[:, cols.start // PER_COL : cols.stop // PER_COL]

        x_codes = sb("x_codes", [P, S], U32)
        for cols in halves:
            nc.vector.tensor_copy(x_codes[:, cols], x_table[:].bitcast(U32).indirect(entries(offs_sb, cols)))

        def first_product(bank, t, cols):
            nc.tensor.matmul_mx(
                out=bank,
                lhsT=w_codes[:, t, :].bitcast(FP8X4),
                lhsT_scale=w_scale[:, t, :],
                rhs=x_codes[:, cols].bitcast(FP8X4),
                rhs_scale=x_scale[4:P, cols],
                start=True,
                stop=True,
            )

        y_early = psum.tile([P, HALF], F32, name="y_early", tag="early")
        y_bank = [psum.tile([P, S], F32, name="y_bank%d" % t, tag="bank%d" % t) for t in range(PACK)]
        first_product(y_early[:], 0, first)
        first_product(y_bank[0][:, second], 0, second)
        for t in range(1, PACK):
            first_product(y_bank[t][:], t, whole)

        bias0 = sb("bias0", [P, 2], F32)
        bias_rest = sb("bias_rest", [P, PACK - 1, 2], F32)
        exp_bias = [bias0[:]] + [bias_rest[:, t, :] for t in range(PACK - 1)]
        top_early = sb("top_early", [P, 1], F32)
        top0 = sb("top0", [P, 1], F32)
        top = sb("top", [P, PACK - 1, 1], F32)

        def y_out(t, top_col):
            nc.vector.tensor_scalar(y[t][:, 0:S], y_bank[t][:], 1.0, None, ALU.mult, ALU.max, accum_out=top_col)

        def biases(engine, dst, t0, t1, tops):
            engine.tensor_tensor(
                dst, neg_tau[:, t0:t1, :], tops.to_broadcast([P, t1 - t0, 2]), ALU.mult
            )

        nc.vector.tensor_scalar(y[0][:, first], y_early[:], 1.0, None, ALU.mult, ALU.max, accum_out=top_early[:])
        nc.vector.tensor_scalar(
            y[0][:, second], y_bank[0][:, second], 1.0, top_early[:], ALU.mult, ALU.max, accum_out=top0[:]
        )
        nc.scalar.activation(bias0[:], neg_tau[:, 0, :], ACT.Copy, scale=top0[:])
        y_out(1, top[:, 0, :])
        y_out(2, top[:, 1, :])
        biases(nc.gpsimd, bias_rest[:, 0:1, :], 1, 2, top[:, 0:1, :])
        y_out(3, top[:, 2, :])
        biases(nc.gpsimd, bias_rest[:, 1:3, :], 2, 4, top[:, 1:3, :])

        gs3 = sb("gs3", [P, PACK], F32)
        nc.gpsimd.tensor_scalar(gs3[:], gs_sb[:], 3.0, 0.0, ALU.mult, ALU.add)

        d_picked = sb("d_picked", [P, H], U32)
        d_codes = sb("d_codes", [P, PACK, P], U32)
        for b in range(2):
            nc.vector.tensor_copy(
                d_picked[:, b * 256 : (b + 1) * 256],
                d_table[:].bitcast(U32).indirect(k1_sb[:, b * 16 : (b + 1) * 16]),
            )
        lo_bias = sb("lo_bias", [P, PACK], F32)
        hi_bias = sb("hi_bias", [P, PACK], F32)

        def deal_words(t0, t1):
            nc.vector.tensor_copy(
                d_codes[:, t0:t1, :].rearrange("p t m -> p m t"),
                d_picked[:].rearrange("p (m t) -> p m t", t=PACK)[:, :, t0:t1],
            )

        deal_words(0, 1)

        h_bank = [psum.tile([P, S], F32, name="h_bank%d" % t, tag="bank0" if t == 0 else "h_bank%d" % t) for t in range(PACK)]

        z_planes = sb("z_planes", [P, PACK, S], BF16)
        ea2g = sb("ea2g", [P, PACK, S], F32, tag="d_table")
        z_grouped = sb("z_grouped", [P, S, PACK], BF16)
        z_codes = sb("z_codes", [P, S], U32)
        z_scale = sb("z_scale", [P, S], U8)
        last = PACK - 1
        ea = [sb("ea%d" % t, [P, S], F32) for t in range(PACK)]
        ea2 = [sb("ea2_%d" % t, [P, S], F32) for t in range(PACK)]

        def exps(t, cols):
            nc.scalar.activation(
                ea2[t][:, cols], y[t][:].indirect(entries(n2_sb, cols)), ACT.Exp,
                bias=exp_bias[t][:, 1:2], scale=tau2_sb[:, t : t + 1],
            )
            nc.scalar.activation(
                ea[t][:, cols], y[t][:].indirect(entries(n1_sb, cols)), ACT.Exp,
                bias=exp_bias[t][:, 0:1], scale=tau_sb[:, t : t + 1],
            )

        def weigh(t, cols):
            nc.vector.tensor_scalar(ea2g[:, t, cols], ea2[t][:, cols], gs3[:, t : t + 1], None, ALU.mult)

        def z_plane(t, cols):
            nc.vector.scalar_tensor_tensor(
                z_planes[:, t, cols], ea[t][:, cols], gs3[:, t : t + 1], ea2g[:, t, cols], ALU.mult, ALU.subtract
            )

        def interleave(cols):
            nc.vector.tensor_copy(z_grouped[:, cols, :], z_planes[:, :, cols].rearrange("p t j -> p j t"))

        def quantise(cols):
            nc.vector.quantize_mx(
                out=z_codes[:, cols].bitcast(FP8X4),
                scales=z_scale[:, cols],
                in_=z_grouped[:, cols, :].rearrange("p j t -> p (j t)"),
            )

        def second_product(bank, t, cols):
            nc.tensor.matmul_mx(
                out=bank,
                lhsT=d_codes[:, t, :].bitcast(FP8X4),
                lhsT_scale=d_scale_plane[:, t * P : (t + 1) * P],
                rhs=z_codes[:, cols].bitcast(FP8X4),
                rhs_scale=z_scale[:, cols],
                start=True,
                stop=True,
            )

        def h_out(t, cols, bank):
            nc.vector.tensor_scalar(h[t][:, cols], bank, 0.0625, None, ALU.mult)

        third, fourth = slice(HALF, HALF + 64), slice(HALF + 64, S)
        exps(0, whole)
        exps(1, whole)
        exps(2, first)
        exps(3, first)
        exps(2, second)
        exps(3, third)
        exps(3, fourth)
        for t in (0, 1):
            diff = sb("diff%d" % t, [P, S], F32)
            nc.gpsimd.tensor_tensor(diff[:], ea[t][:], ea2[t][:], ALU.subtract)
            nc.gpsimd.tensor_scalar(z_planes[:, t, :], diff[:], gs3[:, t : t + 1], 0.0, ALU.mult, ALU.add)
        weigh(2, first)
        weigh(3, first)
        z_plane(2, first)
        z_plane(3, first)
        weigh(2, second)
        interleave(first)
        z_plane(2, second)
        quantise(first)
        h_early = psum.tile([P, HALF], F32, name="h_early", tag="early")
        second_product(h_early[:], 0, first)
        weigh(3, third)
        z_plane(3, third)
        weigh(3, fourth)
        interleave(third)
        z_plane(3, fourth)
        quantise(third)
        interleave(fourth)
        h_out(0, first, h_early[:])
        quantise(fourth)
        second_product(h_bank[0][:, second], 0, second)
        nc.vector.scalar_tensor_tensor(lo_bias[:], lo_sb[:], -1.0, sl_sb[:], ALU.mult, ALU.mult)
        nc.vector.scalar_tensor_tensor(hi_bias[:], hi_sb[:], -1.0, sl_sb[:], ALU.mult, ALU.mult)
        deal_words(1, PACK)
        for t in range(1, PACK):
            second_product(h_bank[t][:], t, whole)
        h_out(0, second, h_bank[0][:, second])
        for t in range(1, PACK):
            h_out(t, whole, h_bank[t][:])

        out_rows = out.rearrange("(p t) j -> p t j", t=PACK)

        def finish(t, cols, sg, sg2):
            width = cols.stop - cols.start
            band = sb("band%d_%d" % (t, cols.start), [P, width], F32)
            res = sb("res%d_%d" % (t, cols.start), [P, width], F32)
            nc.vector.tensor_tensor(band[:], sg[:, cols], sg2[:, cols], ALU.subtract)
            nc.vector.tensor_tensor(res[:], band[:], h[t][:, cols], ALU.mult)
            nc.sync.dma_start(out_rows[:, t, cols], res[:])

        for t in range(PACK):
            sg = sb("sg%d" % t, [P, S], F32)
            sg2 = sb("sg2_%d" % t, [P, S], F32)
            for cols in (halves if t == last else [whole]):
                nc.scalar.activation(
                    sg[:, cols], h[t][:].indirect(entries(n3_sb, cols)), ACT.Sigmoid,
                    bias=lo_bias[:, t : t + 1], scale=sl_sb[:, t : t + 1],
                )
                nc.scalar.activation(
                    sg2[:, cols], h[t][:].indirect(entries(n3_sb, cols)), ACT.Sigmoid,
                    bias=hi_bias[:, t : t + 1], scale=sl_sb[:, t : t + 1],
                )
                finish(t, cols, sg, sg2)
